import numpy as np, ml_dtypes
CORES = [5,29,101,125,133,157,229,253]
N = 8
import mx_ref
BF = ml_dtypes.bfloat16
def entries(a):
    return np.ascontiguousarray(a.T).reshape(-1)
def table(e):
    return np.ascontiguousarray(np.reshape(e, (-1, 16)).T).astype(np.int32)
def cut(t, i, w=512):
    return t[:, w * i:w * i + w]
def decode(q):
    o = []
    for b in range(4):
        e = np.zeros((128, 128, 4), np.float32); e[np.arange(128), np.arange(128), b] = 1
        o.append(mx_ref.matmul(mx_ref.quantize(e.reshape(128, 512).astype(BF)), q))
    return np.stack(o, axis=2).reshape(128, -1)
def f(rng, *shape):
    return mx_ref.flush((rng.standard_normal(shape, dtype=np.float32) * np.exp2(rng.integers(-2, 3, shape[:-1] + (1,)))).astype(BF))
def wide(rng, *shape, cols=0):
    v = rng.standard_normal(shape, dtype=np.float32) * np.exp2(rng.integers(-12, 13, shape)).astype(np.float32)
    if cols: v *= np.repeat(np.exp2(rng.integers(-cols, cols + 1, shape[:-2] + (1, shape[-1] // 4))) * (rng.random(shape[:-2] + (1, shape[-1] // 4)) > 0.0625), 4, axis=-1).astype(np.float32)
    return mx_ref.flush(v.astype(BF))
T, K, O = 256, 256, 1
HA = (1237, 1811, 947, 1543, 2017, 733, 1409, 1699)
HB = (40503, 12289, 58111, 3571, 27644, 61007, 19211, 50021)
def setup_inputs(rng):
    return {"tb": f(rng, N, 128, 4 * K), "ids": np.stack([table(rng.integers(0, 4096, T)) for r in range(N)]), "w": f(rng, N, 128, 512 * O)}
def setup_inputs_alike(rng):
    d = setup_inputs(rng); e = rng.integers(0, 4096, T)
    d["ids"] = np.stack([table(e) for r in range(N)]); return d
def setup_inputs_ends(rng):
    d = setup_inputs(rng); o = []
    for r in range(N):
        e = rng.choice([0, 4095], T); e[rng.permutation(T)[:2]] = [0, 4095]
        o.append(table(e))
    d["ids"] = np.stack(o); return d
def setup_inputs_order(rng):
    d = setup_inputs(rng); t = rng.standard_normal((N, 128, 4 * K), dtype=np.float32)
    one = rng.permutation(np.concatenate([np.arange(N), rng.integers(0, N, 16 - N)]))
    for g in range(16):
        p = int(one[g]); o = int(rng.choice([q for q in range(N) if abs(q - p) >= 2]))
        size = np.float32(2.0 ** int(rng.integers(0, 3)))
        X = np.tile(rng.choice([-1, 1], (8, 4)).astype(np.float32) * size, (1, K))
        v = t[:, 8 * g:8 * g + 8]; v *= size * np.float32(2.0 ** -14)
        v[min(p, o)] = X; v[max(p, o)] = -X
    d["tb"] = mx_ref.flush(t.astype(BF)); return d
def setup_inputs_same(rng):
    d = setup_inputs(rng)
    d["ids"] = np.stack([table(np.full(T, rng.integers(0, 4096))) for r in range(N)]); return d
def setup_inputs_spread(rng):
    d = setup_inputs(rng); d["tb"] = wide(rng, N, 128, 4 * K, cols=8); return d
def check_inputs(d):
    b = []
    for r in range(N):
        e = entries(d["ids"][r])
        if e.min() < 0 or e.max() > 4095: b.append("ids")
    return b
def address(q, e):
    return ((e * HA[q] + HB[q]) >> 5) & (K - 1)
def reference(tb, ids, w):
    d = [decode(mx_ref.quantize(tb[q])).reshape(128, -1, 4) for q in range(N)]
    y = np.zeros((N, 128, O * T), np.float32)
    for r in range(N):
        e = entries(ids[r])
        v = d[0][:, address(0, e)]
        for q in range(1, N): v = v + d[q][:, address(q, e)]
        V = mx_ref.quantize(np.ascontiguousarray(v.reshape(128, -1)).astype(BF))
        for o in range(O): y[r][:, T * o:T * o + T] = mx_ref.matmul(mx_ref.quantize(np.ascontiguousarray(cut(w[r], o))), V)
    return {"y": y}

@@ -1,0 +1,212 @@
+from concourse.bass import DstId, RemoteDMATransfer
+from concourse.mybir import dt, AluOpType, ActivationFunctionType
+
+N, TOK, K, MAXC = 8, 256, 256, 512
+HA = (1237, 1811, 947, 1543, 2017, 733, 1409, 1699)
+HB = (40503, 12289, 58111, 3571, 27644, 61007, 19211, 50021)
+
+SCRATCH = {
+    "codes": ("sbuf", [128, N * K], "float8_e4m3fn_x4"),
+    "planes": ("sbuf", [128, N * K], "uint8"),
+    "tt": ("sbuf", [128, 4 * K], "bfloat16"),
+    "wt": ("sbuf", [128, 512], "bfloat16"),
+    "wc": ("sbuf", [128, 128], "float8_e4m3fn_x4"),
+    "wp": ("sbuf", [128, 128], "uint8"),
+    "ones": ("sbuf", [128, 516], "bfloat16"),
+    "hot": ("sbuf", [128, 516], "bfloat16"),
+    "ec": ("sbuf", [128, 512], "float8_e4m3fn_x4"),
+    "ep": ("sbuf", [128, 512], "uint8"),
+    "idl": ("sbuf", [128, TOK // 16], "int32"),
+    "hx": ("sbuf", [128, N * TOK // 16], "int32"),
+    "hc": ("sbuf", [128, N * TOK // 16], "int32"),
+    "off": ("sbuf", [128, N * 4 * TOK // 16], "uint16"),
+    "dd": ("sbuf", [128, N * 4 * K], "bfloat16"),
+    "acc": ("sbuf", [128, 4 * TOK], "float32"),
+    "vt": ("sbuf", [128, 4 * TOK], "bfloat16"),
+    "vc": ("sbuf", [128, TOK], "float8_e4m3fn_x4"),
+    "vp": ("sbuf", [128, TOK], "uint8"),
+    "yt": ("sbuf", [128, TOK], "float32"),
+    "ps": ("psum", [128, 8 * 512], "float32"),
+}
+SEMAPHORES = (["s_tb", "s_ids", "s_w", "s_ones", "s_hot", "s_qt", "s_qe", "s_hx", "s_hc", "s_off", "s_qw", "s_out",
+               "r_codes", "r_plane", "r_sent"]
+              + ["arr%d" % q for q in range(N)] + ["cp%d" % q for q in range(N)] + ["add%d" % q for q in range(N)]
+              + ["mm%d_%d" % (q, b) for q in range(N) for b in range(4)]
+              + ["l%d" % h for h in range(2)] + ["qv%d" % h for h in range(2)]
+              + ["ym%d" % h for h in range(2)] + ["yc%d" % h for h in range(2)])
+
+
+def routes(core, T, topo):
+    same = [d for d in T.cores if d != core and topo.may_write(core, d)]
+    other = [d for d in T.cores if not topo.may_write(core, d)]
+    owners = [x for x in topo.cores_of(core) if x != core and all(topo.may_write(x, d) for d in other)]
+    near = [x for x in owners if topo.die(x) == topo.die(core)]
+    far = [x for x in owners if topo.die(x) != topo.die(core)]
+    relays = [near[0], far[0]]
+    plane = sorted(same + [core])
+    me = plane.index(core)
+    same = plane[me + 1:] + plane[:me]
+    turn = [other[(me + k) % len(other)] for k in range(len(other))]
+    return same, relays, [turn[0::2], turn[1::2]] if me % 2 == 0 else [turn[0::2], turn[1::2]]
+
+
+def ids_of(src, dsts, topo):
+    out = []
+    for d in dsts:
+        rid, pid = topo.addr(d, src)
+        out.append(DstId(rid=rid, pnc=pid))
+    return out
+
+
+def common(src, dsts, topo):
+    m = topo.mask(src, dsts[0])
+    for d in dsts:
+        m &= topo.mask(src, d)
+    return m
+
+
+def count(m):
+    return bin(m).count("1")
+
+
+def copy_to(g, src, dsts, ap, remote_sem, local_sem, topo):
+    m = common(src, dsts, topo)
+    g.remote_dma_fused([RemoteDMATransfer(dst_ids=ids_of(src, dsts, topo), dma_engine_mask=m, remote_sem=remote_sem,
+                                          srcs=[ap], dsts=[ap] * len(dsts))], local_sem=local_sem)
+    return count(m)
+
+
+def table(T, q):
+    return T.codes[:, K * q:K * q + K], T.planes[:, K * q:K * q + K]
+
+
+def relay_program(g, core, rank, dsts, T, topo):
+    home = T.cores[rank]
+    c, p = table(T, rank)
+    n = count(topo.mask(home, core))
+    S = T.sem
+    sent = 0
+    g.wait_ge(S.r_codes, n)
+    sent += copy_to(g, core, dsts, c.bitcast(dt.uint8), S["arr%d" % rank], S.r_sent, topo)
+    g.wait_ge(S.r_plane, n)
+    sent += copy_to(g, core, dsts, p, S["arr%d" % rank], S.r_sent, topo)
+    g.wait_ge(S.r_sent, sent)
+
+
+def rank_program(g, core, T, topo):
+    rank = T.rank_of(core)
+    if rank is None:
+        for q, home in enumerate(T.cores):
+            if core in topo.cores_of(home):
+                same, relays, parts = routes(home, T, topo)
+                if core in relays:
+                    relay_program(g, core, q, parts[relays.index(core)], T, topo)
+        return
+    S = T.sem
+    same, relays, parts = routes(core, T, topo)
+    L = TOK // 16
+    order = [rank] + [q for q in range(N) if q != rank]
+
+    need = {}
+    for q, home in enumerate(T.cores):
+        if home == core:
+            continue
+        s2, r2, p2 = routes(home, T, topo)
+        if core in s2:
+            need[q] = 2 * count(common(home, s2, topo))
+        else:
+            i = 0 if core in p2[0] else 1
+            need[q] = 2 * count(common(r2[i], p2[i], topo))
+
+    g.sync.dma_start(T.tt[:], T.tb[:]).then_inc(S.s_tb, 16)
+    for k in range(8):
+        g.scalar.dma_start(T.idl[16 * k:16 * k + 16, :], T.ids[:]).then_inc(S.s_ids, 16)
+    g.sync.dma_start(T.wt[:], T.w[:]).then_inc(S.s_w, 16)
+
+    g.wait_ge(S.s_ones, 1)
+    g.affine_select(T.hot[:], T.ones[:], [[-1, 516]], AluOpType.is_equal, 0.0, 3, 4).then_inc(S.s_hot, 1)
+    c, p = table(T, rank)
+    g.wait_ge(S.s_qt, 1)
+    sent = copy_to(g, core, relays, c.bitcast(dt.uint8), S.r_codes, S.r_sent, topo)
+    sent += copy_to(g, core, relays, p, S.r_plane, S.r_sent, topo)
+    sent += copy_to(g, core, same, c.bitcast(dt.uint8), S["arr%d" % rank], S.r_sent, topo)
+    sent += copy_to(g, core, same, p, S["arr%d" % rank], S.r_sent, topo)
+    g.wait_ge(S.r_sent, sent)
+
+    v = g.vector
+    v.memset(T.ones[:], 1.0).then_inc(S.s_ones, 1)
+    v.wait_ge(S.s_tb, 16)
+    v.quantize_mx(c, p, T.tt[:]).then_inc(S.s_qt, 1)
+    v.wait_ge(S.s_hot, 1)
+    for b in range(4):
+        v.quantize_mx(T.ec[:, 128 * b:128 * b + 128], T.ep[:, 128 * b:128 * b + 128], T.hot[:, 3 - b:3 - b + 512]).then_inc(S.s_qe, 1)
+    v.wait_ge(S.s_ids, 128)
+    for q in range(N):
+        v.tensor_scalar(T.hx[:, L * q:L * q + L], T.idl[:], HA[q], HB[q], AluOpType.mult, AluOpType.add).then_inc(S.s_hx, 1)
+    v.wait_ge(S.s_hx, N)
+    v.tensor_scalar(T.hc[:], T.hx[:], 5, K - 1, AluOpType.logical_shift_right, AluOpType.bitwise_and).then_inc(S.s_hc, 1)
+    v.wait_ge(S.s_hc, 1)
+    for q in range(N):
+        for t in range(4):
+            a = 4 * L * q + L * t
+            v.tensor_scalar(T.off[:, a:a + L], T.hc[:, L * q:L * q + L], K * t, None, AluOpType.add).then_inc(S.s_off, 1)
+    v.wait_ge(S.s_w, 16)
+    v.quantize_mx(T.wc[:], T.wp[:], T.wt[:]).then_inc(S.s_qw, 1)
+    v.wait_ge(S.s_off, 4 * N)
+
+    for k, q in enumerate(order):
+        qc, qp = table(T, q)
+        if q == rank:
+            g.tensor.wait_ge(S.s_qt, 1)
+            g.tensor.wait_ge(S.s_qe, 4)
+        else:
+            g.tensor.wait_ge(S["arr%d" % q], need[q])
+        if k >= 2:
+            g.tensor.wait_ge(S["cp%d" % order[k - 2]], 4)
+        for b in range(4):
+            a = 512 * (4 * (k % 2) + b)
+            g.tensor.matmul_mx(T.ps[:, a:a + K], T.ec[:, 128 * b:128 * b + 128], T.ep[:, 128 * b:128 * b + 128],
+                               qc, qp, True, True).then_inc(S["mm%d_%d" % (q, b)], 1)
+
+    for k, q in enumerate(order):
+        for b in range(4):
+            a = 512 * (4 * (k % 2) + b)
+            g.scalar.wait_ge(S["mm%d_%d" % (q, b)], 1)
+            d = 4 * K * q + K * b
+            g.scalar.activation(T.dd[:, d:d + K], T.ps[:, a:a + K], ActivationFunctionType.Copy).then_inc(S["cp%d" % q], 1)
+
+    for q in range(N - 1):
+        v.wait_ge(S["cp%d" % q], 4)
+        win = T.dd[:, 4 * K * q:4 * K * q + 4 * K].indirect(T.off[:, 4 * L * q:4 * L * q + 4 * L])
+        if q == 0:
+            v.tensor_copy(T.acc[:], win).then_inc(S["add%d" % q], 1)
+        else:
+            v.wait_ge(S["add%d" % (q - 1)], 1)
+            v.tensor_tensor(T.acc[:], win, T.acc[:], AluOpType.add).then_inc(S["add%d" % q], 1)
+    q = N - 1
+    H, HL = TOK // 2, L // 2
+    v.wait_ge(S["cp%d" % q], 4)
+    v.wait_ge(S["add%d" % (q - 1)], 1)
+    for h in range(2):
+        for t in range(4):
+            a = 4 * L * q + L * t + HL * h
+            win = T.dd[:, 4 * K * q:4 * K * q + 4 * K].indirect(T.off[:, a:a + HL])
+            v.tensor_tensor(T.vt[:, 4 * H * h + t:4 * H * h + 4 * H:4], win, T.acc[:, TOK * t + H * h:TOK * t + H * h + H],
+                            AluOpType.add).then_inc(S["l%d" % h], 1)
+        v.wait_ge(S["l%d" % h], 4)
+        v.quantize_mx(T.vc[:, H * h:H * h + H], T.vp[:, H * h:H * h + H], T.vt[:, 4 * H * h:4 * H * h + 4 * H]).then_inc(S["qv%d" % h], 1)
+
+    g.tensor.wait_ge(S.s_qw, 1)
+    g.tensor.wait_ge(S["cp%d" % order[N - 2]], 4)
+    for h in range(2):
+        g.tensor.wait_ge(S["qv%d" % h], 1)
+        g.tensor.matmul_mx(T.ps[:, 512 * h:512 * h + H], T.wc[:], T.wp[:], T.vc[:, H * h:H * h + H], T.vp[:, H * h:H * h + H],
+                           True, True).then_inc(S["ym%d" % h], 1)
+    g.scalar.wait_ge(S.ym0, 1)
+    g.scalar.activation(T.yt[:, 0:H], T.ps[:, 0:H], ActivationFunctionType.Copy).then_inc(S.yc0, 1)
+    v.wait_ge(S.ym1, 1)
+    v.tensor_copy(T.yt[:, H:TOK], T.ps[:, 512:512 + H]).then_inc(S.yc1, 1)
+    for h in range(2):
+        g.sync.wait_ge(S["yc%d" % h], 1)
+        g.sync.dma_start(T.y[:, H * h:H * h + H], T.yt[:, H * h:H * h + H]).then_inc(S.s_out, 16)
+    g.sync.wait_ge(S.s_out, 32)

@@ -1,9 +1,12 @@
 from concourse.bass import DstId, RemoteDMATransfer
 from concourse.mybir import dt, AluOpType, ActivationFunctionType
 
-N, TOK, K, MAXC = 8, 256, 256, 512
+N, TOK, K = 8, 256, 256
 HA = (1237, 1811, 947, 1543, 2017, 733, 1409, 1699)
 HB = (40503, 12289, 58111, 3571, 27644, 61007, 19211, 50021)
+HT = TOK // 2
+L = HT // 16
+UNITS = 6
 
 SCRATCH = {
     "codes": ("sbuf", [128, N * K], "float8_e4m3fn_x4"),
@@ -17,45 +20,64 @@ SCRATCH = {
     "ec": ("sbuf", [128, 512], "float8_e4m3fn_x4"),
     "ep": ("sbuf", [128, 512], "uint8"),
     "idl": ("sbuf", [128, TOK // 16], "int32"),
-    "hx": ("sbuf", [128, N * TOK // 16], "int32"),
-    "hc": ("sbuf", [128, N * TOK // 16], "int32"),
-    "off": ("sbuf", [128, N * 4 * TOK // 16], "uint16"),
+    "id4": ("sbuf", [128, 4 * L], "int32"),
+    "hx": ("sbuf", [128, N * 4 * L], "int32"),
+    "hc": ("sbuf", [128, N * 4 * L], "int32"),
+    "cst": ("sbuf", [128, N * 4 * L], "int32"),
+    "ofs": ("sbuf", [128, N * 4 * L], "int32"),
+    "off": ("sbuf", [128, N * 4 * L], "uint16"),
     "dd": ("sbuf", [128, N * 4 * K], "bfloat16"),
-    "acc": ("sbuf", [128, 4 * TOK], "float32"),
-    "vt": ("sbuf", [128, 4 * TOK], "bfloat16"),
+    "acc": ("sbuf", [128, 4 * HT], "float32"),
+    "vt": ("sbuf", [128, 4 * HT], "bfloat16"),
     "vc": ("sbuf", [128, TOK], "float8_e4m3fn_x4"),
     "vp": ("sbuf", [128, TOK], "uint8"),
     "yt": ("sbuf", [128, TOK], "float32"),
     "ps": ("psum", [128, 8 * 512], "float32"),
 }
-SEMAPHORES = (["s_tb", "s_ids", "s_w", "s_ones", "s_hot", "s_qt", "s_qe", "s_hx", "s_hc", "s_off", "s_qw", "s_out",
-               "r_codes", "r_plane", "r_sent"]
-              + ["arr%d" % q for q in range(N)] + ["cp%d" % q for q in range(N)] + ["add%d" % q for q in range(N)]
-              + ["mm%d_%d" % (q, b) for q in range(N) for b in range(4)]
-              + ["l%d" % h for h in range(2)] + ["qv%d" % h for h in range(2)]
-              + ["ym%d" % h for h in range(2)] + ["yc%d" % h for h in range(2)])
+SEMAPHORES = (["s_tb", "s_ids", "s_w", "s_ones", "s_hot", "s_cst", "s_qt", "s_qe", "s_id4", "s_hx", "s_hc", "s_ofs", "s_off",
+               "s_qw", "s_o0", "s_o1", "r_ids", "r_codes", "r_plane", "r_sent", "r_v", "lv", "qv", "ym0", "ym1", "yc0", "yc1"]
+              + ["arr%d" % q for q in range(N)] + ["add%d" % k for k in range(N)]
+              + ["fw%d" % u for u in range(UNITS)] + ["cu%d" % u for u in range(UNITS)]
+              + ["mm%d_%d" % (u, b) for u in range(UNITS) for b in range(4)])
 
 
-def routes(core, T, topo):
-    same = [d for d in T.cores if d != core and topo.may_write(core, d)]
-    other = [d for d in T.cores if not topo.may_write(core, d)]
-    owners = [x for x in topo.cores_of(core) if x != core and all(topo.may_write(x, d) for d in other)]
-    near = [x for x in owners if topo.die(x) == topo.die(core)]
-    far = [x for x in owners if topo.die(x) != topo.die(core)]
-    relays = [near[0], far[0]]
-    plane = sorted(same + [core])
-    me = plane.index(core)
-    same = plane[me + 1:] + plane[:me]
-    turn = [other[(me + k) % len(other)] for k in range(len(other))]
-    return same, relays, [turn[0::2], turn[1::2]] if me % 2 == 0 else [turn[0::2], turn[1::2]]
+def planes_of(T, topo):
+    a = [q for q in range(N) if q == 0 or topo.same_plane(T.cores[0], T.cores[q])]
+    return a, [q for q in range(N) if q not in a]
 
 
-def ids_of(src, dsts, topo):
-    out = []
-    for d in dsts:
-        rid, pid = topo.addr(d, src)
-        out.append(DstId(rid=rid, pnc=pid))
-    return out
+def sides(rank, T, topo):
+    a, b = planes_of(T, topo)
+    return (a, b) if rank in a else (b, a)
+
+
+def relays_of(rank, T, topo):
+    home = T.cores[rank]
+    mine, other = sides(rank, T, topo)
+    owners = [x for x in topo.cores_of(home) if x != home and all(topo.may_write(x, T.cores[d]) for d in other)]
+    near = [x for x in owners if topo.die(x) == topo.die(home)]
+    far = [x for x in owners if topo.die(x) != topo.die(home)]
+    return near[0], far[0]
+
+
+def helper(rank, T, topo):
+    return relays_of(rank, T, topo)[0]
+
+
+def direct(rank, T, topo):
+    mine, other = sides(rank, T, topo)
+    me = mine.index(rank)
+    return [helper(mine[me ^ x], T, topo) for x in (1, 2, 3)]
+
+
+def relayed(rank, T, topo):
+    mine, other = sides(rank, T, topo)
+    me = mine.index(rank)
+    return [[helper(other[me ^ x], T, topo) for x in xs] for xs in ((0, 1), (2, 3))]
+
+
+def count(m):
+    return bin(m).count("1")
 
 
 def common(src, dsts, topo):
@@ -65,148 +87,239 @@ def common(src, dsts, topo):
     return m
 
 
-def count(m):
-    return bin(m).count("1")
-
-
-def copy_to(g, src, dsts, ap, remote_sem, local_sem, topo):
+def copy_to(g, src, dsts, out, in_, remote_sem, local_sem, topo):
     m = common(src, dsts, topo)
-    g.remote_dma_fused([RemoteDMATransfer(dst_ids=ids_of(src, dsts, topo), dma_engine_mask=m, remote_sem=remote_sem,
-                                          srcs=[ap], dsts=[ap] * len(dsts))], local_sem=local_sem)
+    ids = []
+    for d in dsts:
+        rid, pid = topo.addr(d, src)
+        ids.append(DstId(rid=rid, pnc=pid))
+    g.remote_dma_fused([RemoteDMATransfer(dst_ids=ids, dma_engine_mask=m, remote_sem=remote_sem,
+                                          srcs=[in_], dsts=[out] * len(dsts))], local_sem=local_sem)
     return count(m)
 
 
-def table(T, q):
-    return T.codes[:, K * q:K * q + K], T.planes[:, K * q:K * q + K]
+def slot_of(q, T, topo):
+    a, b = planes_of(T, topo)
+    return (a + b).index(q)
 
 
-def relay_program(g, core, rank, dsts, T, topo):
-    home = T.cores[rank]
-    c, p = table(T, rank)
-    n = count(topo.mask(home, core))
+def slots(T, s, n):
+    return T.codes[:, K * s:K * s + K * n], T.planes[:, K * s:K * s + K * n]
+
+
+def send_slots(g, src, dsts, T, s, n, sem, topo):
+    c, p = slots(T, s, n)
+    k = copy_to(g, src, dsts, p, p, sem, T.sem.r_sent, topo)
+    return k + copy_to(g, src, dsts, c.bitcast(dt.uint8), c.bitcast(dt.uint8), sem, T.sem.r_sent, topo)
+
+
+def relay(g, core, rank, dsts, T, topo):
     S = T.sem
-    sent = 0
-    g.wait_ge(S.r_codes, n)
-    sent += copy_to(g, core, dsts, c.bitcast(dt.uint8), S["arr%d" % rank], S.r_sent, topo)
+    c, p = slots(T, slot_of(rank, T, topo), 1)
+    n = count(common(T.cores[rank], relays_of(rank, T, topo), topo))
+    arr = S["arr%d" % rank]
     g.wait_ge(S.r_plane, n)
-    sent += copy_to(g, core, dsts, p, S["arr%d" % rank], S.r_sent, topo)
-    g.wait_ge(S.r_sent, sent)
+    sent = copy_to(g, core, dsts, p, p, arr, S.r_sent, topo)
+    g.wait_ge(S.r_codes, n)
+    return sent + copy_to(g, core, dsts, c.bitcast(dt.uint8), c.bitcast(dt.uint8), arr, S.r_sent, topo)
 
 
 def rank_program(g, core, T, topo):
     rank = T.rank_of(core)
-    if rank is None:
-        for q, home in enumerate(T.cores):
-            if core in topo.cores_of(home):
-                same, relays, parts = routes(home, T, topo)
-                if core in relays:
-                    relay_program(g, core, q, parts[relays.index(core)], T, topo)
+    if rank is not None:
+        lookup_core(g, core, rank, True, T, topo)
         return
+    for q, home in enumerate(T.cores):
+        if core in topo.cores_of(home):
+            H, F = relays_of(q, T, topo)
+            if core == H:
+                lookup_core(g, core, q, False, T, topo)
+            elif core == F:
+                sent = relay(g, core, q, relayed(q, T, topo)[1], T, topo)
+                g.wait_ge(T.sem.r_sent, sent)
+
+
+def lookup_core(g, core, rank, is_rank, T, topo):
     S = T.sem
-    same, relays, parts = routes(core, T, topo)
-    L = TOK // 16
-    order = [rank] + [q for q in range(N) if q != rank]
+    v = g.vector
+    home = T.cores[rank]
+    H, F = relays_of(rank, T, topo)
+    mine, other = sides(rank, T, topo)
+    me = mine.index(rank)
+    o = 2 - 2 * (me // 2)
+    units = [[rank], [mine[me ^ 1]], mine[o:o + 2], [other[0]], [other[1]], other[2:4]]
+    ufirst = [slot_of(u[0], T, topo) for u in units]
+    n16 = count(topo.mask(H, home))
 
     need = {}
-    for q, home in enumerate(T.cores):
-        if home == core:
+    for q in range(N):
+        if q == rank:
             continue
-        s2, r2, p2 = routes(home, T, topo)
-        if core in s2:
-            need[q] = 2 * count(common(home, s2, topo))
+        if H in direct(q, T, topo):
+            need[q] = 2 * count(common(T.cores[q], direct(q, T, topo), topo))
         else:
-            i = 0 if core in p2[0] else 1
-            need[q] = 2 * count(common(r2[i], p2[i], topo))
+            i = 0 if H in relayed(q, T, topo)[0] else 1
+            need[q] = 2 * count(common(relays_of(q, T, topo)[i], relayed(q, T, topo)[i], topo))
 
-    g.sync.dma_start(T.tt[:], T.tb[:]).then_inc(S.s_tb, 16)
-    for k in range(8):
-        g.scalar.dma_start(T.idl[16 * k:16 * k + 16, :], T.ids[:]).then_inc(S.s_ids, 16)
-    g.sync.dma_start(T.wt[:], T.w[:]).then_inc(S.s_w, 16)
+    single = [q for u in units if len(u) == 1 for q in u]
+    paired = [q for u in units if len(u) == 2 for q in u]
+    pos = {q: i for i, q in enumerate(single + paired)}
+    win, unit_of = {}, {}
+    for u, qs in enumerate(units):
+        base = 4 * K * pos[qs[0]]
+        for i, q in enumerate(qs):
+            win[q] = (base + K * i, base + 4 * K * len(qs))
+            unit_of[q] = u
+
+    if is_rank:
+        g.sync.dma_start(T.tt[:], T.tb[:]).then_inc(S.s_tb, 16)
+        for k in range(8):
+            eng = g.scalar if k < 6 else g.sync
+            eng.dma_start(T.idl[16 * k:16 * k + 16, :], T.ids[:]).then_inc(S.s_ids, 16)
+        g.sync.dma_start(T.wt[:], T.w[:]).then_inc(S.s_w, 16)
+
+    def parts():
+        for i in range(2):
+            a = 4 * 4 * L * i
+            g.iota(T.cst[:, a:a + 16 * L], [[0, 4], [K * (i + 1), 4], [0, L]], 0, 0).then_inc(S.s_cst, 1)
 
     g.wait_ge(S.s_ones, 1)
     g.affine_select(T.hot[:], T.ones[:], [[-1, 516]], AluOpType.is_equal, 0.0, 3, 4).then_inc(S.s_hot, 1)
-    c, p = table(T, rank)
-    g.wait_ge(S.s_qt, 1)
-    sent = copy_to(g, core, relays, c.bitcast(dt.uint8), S.r_codes, S.r_sent, topo)
-    sent += copy_to(g, core, relays, p, S.r_plane, S.r_sent, topo)
-    sent += copy_to(g, core, same, c.bitcast(dt.uint8), S["arr%d" % rank], S.r_sent, topo)
-    sent += copy_to(g, core, same, p, S["arr%d" % rank], S.r_sent, topo)
-    g.wait_ge(S.r_sent, sent)
+    if is_rank:
+        c, p = slots(T, ufirst[0], 1)
+        g.wait_ge(S.s_ids, 128)
+        sent = copy_to(g, core, [H], T.idl[:, 0:L], T.idl[:, L:2 * L], S.r_ids, S.r_sent, topo)
+        g.wait_ge(S.s_qt, 1)
+        sent += copy_to(g, core, [H, F], p, p, S.r_plane, S.r_sent, topo)
+        sent += copy_to(g, core, [H, F], c.bitcast(dt.uint8), c.bitcast(dt.uint8), S.r_codes, S.r_sent, topo)
+        sent += send_slots(g, core, direct(rank, T, topo), T, ufirst[0], 1, S["arr%d" % rank], topo)
+        parts()
+        g.wait_ge(S.r_sent, sent)
+    else:
+        parts()
+        sent = relay(g, core, rank, relayed(rank, T, topo)[0], T, topo)
+        for u in range(1, UNITS):
+            for q in units[u]:
+                g.wait_ge(S["arr%d" % q], need[q])
+            sent += send_slots(g, core, [home], T, ufirst[u], len(units[u]), S["fw%d" % u], topo)
+        g.wait_ge(S.qv, 1)
+        sent += copy_to(g, core, [home], T.vp[:, HT:TOK], T.vp[:, 0:HT], S.r_v, S.r_sent, topo)
+        sent += copy_to(g, core, [home], T.vc[:, HT:TOK].bitcast(dt.uint8), T.vc[:, 0:HT].bitcast(dt.uint8), S.r_v, S.r_sent, topo)
+        g.wait_ge(S.r_sent, sent)
 
-    v = g.vector
     v.memset(T.ones[:], 1.0).then_inc(S.s_ones, 1)
-    v.wait_ge(S.s_tb, 16)
-    v.quantize_mx(c, p, T.tt[:]).then_inc(S.s_qt, 1)
+    if is_rank:
+        v.wait_ge(S.s_tb, 16)
+        v.quantize_mx(c, p, T.tt[:]).then_inc(S.s_qt, 1)
     v.wait_ge(S.s_hot, 1)
     for b in range(4):
         v.quantize_mx(T.ec[:, 128 * b:128 * b + 128], T.ep[:, 128 * b:128 * b + 128], T.hot[:, 3 - b:3 - b + 512]).then_inc(S.s_qe, 1)
-    v.wait_ge(S.s_ids, 128)
+    if is_rank:
+        v.wait_ge(S.s_ids, 128)
+    else:
+        v.wait_ge(S.r_ids, n16)
+    for t in range(4):
+        v.tensor_copy(T.id4[:, L * t:L * t + L], T.idl[:, 0:L]).then_inc(S.s_id4, 1)
+    v.wait_ge(S.s_id4, 4)
+    W = 4 * L
     for q in range(N):
-        v.tensor_scalar(T.hx[:, L * q:L * q + L], T.idl[:], HA[q], HB[q], AluOpType.mult, AluOpType.add).then_inc(S.s_hx, 1)
+        v.tensor_scalar(T.hx[:, W * pos[q]:W * pos[q] + W], T.id4[:], HA[q], HB[q], AluOpType.mult, AluOpType.add).then_inc(S.s_hx, 1)
     v.wait_ge(S.s_hx, N)
     v.tensor_scalar(T.hc[:], T.hx[:], 5, K - 1, AluOpType.logical_shift_right, AluOpType.bitwise_and).then_inc(S.s_hc, 1)
     v.wait_ge(S.s_hc, 1)
-    for q in range(N):
-        for t in range(4):
-            a = 4 * L * q + L * t
-            v.tensor_scalar(T.off[:, a:a + L], T.hc[:, L * q:L * q + L], K * t, None, AluOpType.add).then_inc(S.s_off, 1)
-    v.wait_ge(S.s_w, 16)
-    v.quantize_mx(T.wc[:], T.wp[:], T.wt[:]).then_inc(S.s_qw, 1)
-    v.wait_ge(S.s_off, 4 * N)
+    v.wait_ge(S.s_cst, 2)
+    v.tensor_tensor(T.ofs[:], T.hc[:], T.cst[:], AluOpType.add).then_inc(S.s_ofs, 1)
+    v.wait_ge(S.s_ofs, 1)
+    v.tensor_copy(T.off[:], T.ofs[:]).then_inc(S.s_off, 1)
+    if is_rank:
+        v.wait_ge(S.s_w, 16)
+        v.quantize_mx(T.wc[:], T.wp[:], T.wt[:]).then_inc(S.s_qw, 1)
+    v.wait_ge(S.s_off, 1)
 
-    for k, q in enumerate(order):
-        qc, qp = table(T, q)
-        if q == rank:
+    g.tensor.wait_ge(S.s_qe, 4)
+    for u, qs in enumerate(units):
+        if u == 0 and is_rank:
             g.tensor.wait_ge(S.s_qt, 1)
-            g.tensor.wait_ge(S.s_qe, 4)
+        elif u == 0:
+            n = count(common(home, [H, F], topo))
+            g.tensor.wait_ge(S.r_plane, n)
+            g.tensor.wait_ge(S.r_codes, n)
+        elif is_rank:
+            g.tensor.wait_ge(S["fw%d" % u], 2 * n16)
         else:
-            g.tensor.wait_ge(S["arr%d" % q], need[q])
-        if k >= 2:
-            g.tensor.wait_ge(S["cp%d" % order[k - 2]], 4)
+            for q in qs:
+                g.tensor.wait_ge(S["arr%d" % q], need[q])
+        if u >= 2:
+            g.tensor.wait_ge(S["cu%d" % (u - 2)], copies(units, u - 2))
+        uc, up = slots(T, ufirst[u], len(qs))
         for b in range(4):
-            a = 512 * (4 * (k % 2) + b)
-            g.tensor.matmul_mx(T.ps[:, a:a + K], T.ec[:, 128 * b:128 * b + 128], T.ep[:, 128 * b:128 * b + 128],
-                               qc, qp, True, True).then_inc(S["mm%d_%d" % (q, b)], 1)
+            a = 512 * (4 * (u % 2) + b)
+            g.tensor.matmul_mx(T.ps[:, a:a + K * len(qs)], T.ec[:, 128 * b:128 * b + 128], T.ep[:, 128 * b:128 * b + 128],
+                               uc, up, True, True).then_inc(S["mm%d_%d" % (u, b)], 1)
 
-    for k, q in enumerate(order):
-        for b in range(4):
-            a = 512 * (4 * (k % 2) + b)
-            g.scalar.wait_ge(S["mm%d_%d" % (q, b)], 1)
-            d = 4 * K * q + K * b
-            g.scalar.activation(T.dd[:, d:d + K], T.ps[:, a:a + K], ActivationFunctionType.Copy).then_inc(S["cp%d" % q], 1)
+    def bring(eng, u, bs):
+        base = 4 * K * pos[units[u][0]]
+        n = len(units[u])
+        for b in bs[::n]:
+            for x in range(b, b + n):
+                eng.wait_ge(S["mm%d_%d" % (u, x)], 1)
+            a = 512 * (4 * (u % 2) + b)
+            d = base + K * n * b
+            out, in_ = T.dd[:, d:d + K * n * n], T.ps[:, a:a + K * n * n]
+            if eng is v:
+                v.tensor_copy(out, in_).then_inc(S["cu%d" % u], 1)
+            else:
+                eng.activation(out, in_, ActivationFunctionType.Copy).then_inc(S["cu%d" % u], 1)
 
-    for q in range(N - 1):
-        v.wait_ge(S["cp%d" % q], 4)
-        win = T.dd[:, 4 * K * q:4 * K * q + 4 * K].indirect(T.off[:, 4 * L * q:4 * L * q + 4 * L])
-        if q == 0:
-            v.tensor_copy(T.acc[:], win).then_inc(S["add%d" % q], 1)
+    every, low, high = [0, 1, 2, 3], [0, 1], [2, 3]
+    for u, bs in enumerate([every, every, low, low, every, every]):
+        bring(g.scalar, u, bs)
+
+    seq = list(range(N))
+    if seq[1] in mine:
+        seq[0], seq[1] = seq[1], seq[0]
+    bring(v, 2, high)
+    for k, q in enumerate(seq):
+        if k == 1:
+            bring(v, 3, high)
+        a, e = win[q]
+        w = W * pos[q]
+        v.wait_ge(S["cu%d" % unit_of[q]], copies(units, unit_of[q]))
+        if k > 0:
+            v.wait_ge(S["add%d" % (k - 1)], 1)
+        if k == 0:
+            v.tensor_copy(T.acc[:], T.dd[:, a:e].indirect(T.off[:, w:w + W])).then_inc(S["add%d" % k], 1)
+        elif k < N - 1:
+            v.tensor_tensor(T.acc[:], T.dd[:, a:e].indirect(T.off[:, w:w + W]), T.acc[:], AluOpType.add).then_inc(S["add%d" % k], 1)
         else:
-            v.wait_ge(S["add%d" % (q - 1)], 1)
-            v.tensor_tensor(T.acc[:], win, T.acc[:], AluOpType.add).then_inc(S["add%d" % q], 1)
-    q = N - 1
-    H, HL = TOK // 2, L // 2
-    v.wait_ge(S["cp%d" % q], 4)
-    v.wait_ge(S["add%d" % (q - 1)], 1)
-    for h in range(2):
-        for t in range(4):
-            a = 4 * L * q + L * t + HL * h
-            win = T.dd[:, 4 * K * q:4 * K * q + 4 * K].indirect(T.off[:, a:a + HL])
-            v.tensor_tensor(T.vt[:, 4 * H * h + t:4 * H * h + 4 * H:4], win, T.acc[:, TOK * t + H * h:TOK * t + H * h + H],
-                            AluOpType.add).then_inc(S["l%d" % h], 1)
-        v.wait_ge(S["l%d" % h], 4)
-        v.quantize_mx(T.vc[:, H * h:H * h + H], T.vp[:, H * h:H * h + H], T.vt[:, 4 * H * h:4 * H * h + 4 * H]).then_inc(S["qv%d" % h], 1)
+            for t in range(4):
+                v.tensor_tensor(T.vt[:, t:4 * HT:4], T.dd[:, a:e].indirect(T.off[:, w + L * t:w + L * t + L]),
+                                T.acc[:, HT * t:HT * t + HT], AluOpType.add).then_inc(S.lv, 1)
+    v.wait_ge(S.lv, 4)
+    v.quantize_mx(T.vc[:, 0:HT], T.vp[:, 0:HT], T.vt[:]).then_inc(S.qv, 1)
 
+    if not is_rank:
+        return
     g.tensor.wait_ge(S.s_qw, 1)
-    g.tensor.wait_ge(S["cp%d" % order[N - 2]], 4)
+    g.tensor.wait_ge(S["cu%d" % (UNITS - 2)], copies(units, UNITS - 2))
     for h in range(2):
-        g.tensor.wait_ge(S["qv%d" % h], 1)
-        g.tensor.matmul_mx(T.ps[:, 512 * h:512 * h + H], T.wc[:], T.wp[:], T.vc[:, H * h:H * h + H], T.vp[:, H * h:H * h + H],
+        if h == 0:
+            g.tensor.wait_ge(S.qv, 1)
+        else:
+            g.tensor.wait_ge(S.r_v, 2 * n16)
+        g.tensor.matmul_mx(T.ps[:, 512 * h:512 * h + HT], T.wc[:], T.wp[:], T.vc[:, HT * h:HT * h + HT], T.vp[:, HT * h:HT * h + HT],
                            True, True).then_inc(S["ym%d" % h], 1)
-    g.scalar.wait_ge(S.ym0, 1)
-    g.scalar.activation(T.yt[:, 0:H], T.ps[:, 0:H], ActivationFunctionType.Copy).then_inc(S.yc0, 1)
-    v.wait_ge(S.ym1, 1)
-    v.tensor_copy(T.yt[:, H:TOK], T.ps[:, 512:512 + H]).then_inc(S.yc1, 1)
-    for h in range(2):
-        g.sync.wait_ge(S["yc%d" % h], 1)
-        g.sync.dma_start(T.y[:, H * h:H * h + H], T.yt[:, H * h:H * h + H]).then_inc(S.s_out, 16)
-    g.sync.wait_ge(S.s_out, 32)
+    v.wait_ge(S.ym0, 1)
+    v.tensor_copy(T.yt[:, 0:HT], T.ps[:, 0:HT]).then_inc(S.yc0, 1)
+    g.sync.wait_ge(S.yc0, 1)
+    g.sync.dma_start(T.y[:, 0:HT], T.yt[:, 0:HT]).then_inc(S.s_o0, 16)
+    g.scalar.wait_ge(S.ym1, 1)
+    g.scalar.activation(T.yt[:, HT:TOK], T.ps[:, 512:512 + HT], ActivationFunctionType.Copy).then_inc(S.yc1, 1)
+    g.scalar.wait_ge(S.yc1, 1)
+    g.scalar.dma_start(T.y[:, HT:TOK], T.yt[:, HT:TOK]).then_inc(S.s_o1, 16)
+    g.sync.wait_ge(S.s_o0, 16)
+    g.scalar.wait_ge(S.s_o1, 16)
+
+
+def copies(units, u):
+    return 4 // len(units[u])

@@ -6,7 +6,7 @@ HA = (1237, 1811, 947, 1543, 2017, 733, 1409, 1699)
 HB = (40503, 12289, 58111, 3571, 27644, 61007, 19211, 50021)
 HT = TOK // 2
 L = HT // 16
-UNITS = 6
+W = 4 * L
 
 SCRATCH = {
     "codes": ("sbuf", [128, N * K], "float8_e4m3fn_x4"),
@@ -19,13 +19,15 @@ SCRATCH = {
     "hot": ("sbuf", [128, 516], "bfloat16"),
     "ec": ("sbuf", [128, 512], "float8_e4m3fn_x4"),
     "ep": ("sbuf", [128, 512], "uint8"),
+    "ido": ("dram", [128, TOK // 128], "int32"),
+    "idd": ("dram", [128, TOK // 128], "int32"),
     "idl": ("sbuf", [128, TOK // 16], "int32"),
-    "id4": ("sbuf", [128, 4 * L], "int32"),
-    "hx": ("sbuf", [128, N * 4 * L], "int32"),
-    "hc": ("sbuf", [128, N * 4 * L], "int32"),
-    "cst": ("sbuf", [128, N * 4 * L], "int32"),
-    "ofs": ("sbuf", [128, N * 4 * L], "int32"),
-    "off": ("sbuf", [128, N * 4 * L], "uint16"),
+    "id4": ("sbuf", [128, W], "int32"),
+    "hx": ("sbuf", [128, N * W], "int32"),
+    "hc": ("sbuf", [128, N * W], "int32"),
+    "cst": ("sbuf", [128, N * W], "int32"),
+    "ofs": ("sbuf", [128, N * W], "int32"),
+    "off": ("sbuf", [128, N * W], "uint16"),
     "dd": ("sbuf", [128, N * 4 * K], "bfloat16"),
     "acc": ("sbuf", [128, 4 * HT], "float32"),
     "vt": ("sbuf", [128, 4 * HT], "bfloat16"),
@@ -34,11 +36,11 @@ SCRATCH = {
     "yt": ("sbuf", [128, TOK], "float32"),
     "ps": ("psum", [128, 8 * 512], "float32"),
 }
-SEMAPHORES = (["s_tb", "s_ids", "s_w", "s_ones", "s_hot", "s_cst", "s_qt", "s_qe", "s_id4", "s_hx", "s_hc", "s_ofs", "s_off",
+SEMAPHORES = (["s_tb", "s_ido", "s_ids", "s_w", "s_ones", "s_hot", "s_cst", "s_qt", "s_qe", "s_id4", "s_hx", "s_hc", "s_ofs", "s_off",
                "s_qw", "s_o0", "s_o1", "r_ids", "r_codes", "r_plane", "r_sent", "r_v", "lv", "qv", "ym0", "ym1", "yc0", "yc1"]
-              + ["arr%d" % q for q in range(N)] + ["add%d" % k for k in range(N)]
-              + ["fw%d" % u for u in range(UNITS)] + ["cu%d" % u for u in range(UNITS)]
-              + ["mm%d_%d" % (u, b) for u in range(UNITS) for b in range(4)])
+              + ["ac%d" % q for q in range(N)] + ["ap%d" % q for q in range(N)] + ["add%d" % k for k in range(N)]
+              + ["fp%d" % i for i in range(3)] + ["fc%d" % i for i in range(5)] + ["cu%d" % q for q in range(N)]
+              + ["mm%d_%d" % (q, b) for q in range(N) for b in range(4)])
 
 
 def planes_of(T, topo):
@@ -107,21 +109,14 @@ def slots(T, s, n):
     return T.codes[:, K * s:K * s + K * n], T.planes[:, K * s:K * s + K * n]
 
 
-def send_slots(g, src, dsts, T, s, n, sem, topo):
-    c, p = slots(T, s, n)
-    k = copy_to(g, src, dsts, p, p, sem, T.sem.r_sent, topo)
-    return k + copy_to(g, src, dsts, c.bitcast(dt.uint8), c.bitcast(dt.uint8), sem, T.sem.r_sent, topo)
-
-
 def relay(g, core, rank, dsts, T, topo):
     S = T.sem
     c, p = slots(T, slot_of(rank, T, topo), 1)
-    n = count(common(T.cores[rank], relays_of(rank, T, topo), topo))
-    arr = S["arr%d" % rank]
+    n = count(topo.mask(T.cores[rank], core))
     g.wait_ge(S.r_plane, n)
-    sent = copy_to(g, core, dsts, p, p, arr, S.r_sent, topo)
+    sent = copy_to(g, core, dsts, p, p, S["ap%d" % rank], S.r_sent, topo)
     g.wait_ge(S.r_codes, n)
-    return sent + copy_to(g, core, dsts, c.bitcast(dt.uint8), c.bitcast(dt.uint8), arr, S.r_sent, topo)
+    return sent + copy_to(g, core, dsts, c.bitcast(dt.uint8), c.bitcast(dt.uint8), S["ac%d" % rank], S.r_sent, topo)
 
 
 def rank_program(g, core, T, topo):
@@ -147,61 +142,70 @@ def lookup_core(g, core, rank, is_rank, T, topo):
     mine, other = sides(rank, T, topo)
     me = mine.index(rank)
     o = 2 - 2 * (me // 2)
-    units = [[rank], [mine[me ^ 1]], mine[o:o + 2], [other[0]], [other[1]], other[2:4]]
-    ufirst = [slot_of(u[0], T, topo) for u in units]
     n16 = count(topo.mask(H, home))
 
     need = {}
     for q in range(N):
         if q == rank:
             continue
-        if H in direct(q, T, topo):
-            need[q] = 2 * count(common(T.cores[q], direct(q, T, topo), topo))
-        else:
-            i = 0 if H in relayed(q, T, topo)[0] else 1
-            need[q] = 2 * count(common(relays_of(q, T, topo)[i], relayed(q, T, topo)[i], topo))
+        for src, dsts in [(T.cores[q], direct(q, T, topo))] + list(zip(relays_of(q, T, topo), relayed(q, T, topo))):
+            if core in dsts:
+                need[q] = count(common(src, dsts, topo))
 
-    single = [q for u in units if len(u) == 1 for q in u]
-    paired = [q for u in units if len(u) == 2 for q in u]
-    pos = {q: i for i, q in enumerate(single + paired)}
-    win, unit_of = {}, {}
-    for u, qs in enumerate(units):
-        base = 4 * K * pos[qs[0]]
-        for i, q in enumerate(qs):
-            win[q] = (base + K * i, base + 4 * K * len(qs))
-            unit_of[q] = u
+    seq = list(range(N))
+    if seq[1] in mine:
+        seq[0], seq[1] = seq[1], seq[0]
+    order = [rank]
+    order += [q for q in seq if q in mine and q not in order][:1]
+    order += [q for q in seq if q not in order]
+    fplane = [[mine[me ^ 1]], mine[o:o + 2], other]
+    fcodes = [[mine[me ^ 1]], mine[o:o + 2], other[0:1], other[1:2], other[2:4]]
+    fcodes.sort(key=lambda qs: min(order.index(q) for q in qs))
 
     if is_rank:
         g.sync.dma_start(T.tt[:], T.tb[:]).then_inc(S.s_tb, 16)
-        for k in range(8):
-            eng = g.scalar if k < 6 else g.sync
-            eng.dma_start(T.idl[16 * k:16 * k + 16, :], T.ids[:]).then_inc(S.s_ids, 16)
+        g.scalar.dma_start(T.ido[:], T.ids[:]).then_inc(S.s_ido, 16)
+    else:
+        for eng in (g.sync, g.scalar):
+            eng.wait_ge(S.r_ids, n16)
+    for k in range(8):
+        eng = g.scalar if k % 2 == 0 else g.sync
+        eng.dma_start(T.idl[16 * k:16 * k + 16, :], T.ids[:] if is_rank else T.idd[:]).then_inc(S.s_ids, 16)
+    if is_rank:
         g.sync.dma_start(T.wt[:], T.w[:]).then_inc(S.s_w, 16)
 
-    def parts():
-        for i in range(2):
-            a = 4 * 4 * L * i
-            g.iota(T.cst[:, a:a + 16 * L], [[0, 4], [K * (i + 1), 4], [0, L]], 0, 0).then_inc(S.s_cst, 1)
+    def part_starts():
+        g.iota(T.cst[:], [[0, N], [K, 4], [0, L]], 0, 0).then_inc(S.s_cst, 1)
+
+    def send(dsts, ap, sem):
+        return copy_to(g, core, dsts, ap, ap, sem, S.r_sent, topo)
 
     g.wait_ge(S.s_ones, 1)
     g.affine_select(T.hot[:], T.ones[:], [[-1, 516]], AluOpType.is_equal, 0.0, 3, 4).then_inc(S.s_hot, 1)
+    c, p = slots(T, slot_of(rank, T, topo), 1)
+    cb = c.bitcast(dt.uint8)
     if is_rank:
-        c, p = slots(T, ufirst[0], 1)
-        g.wait_ge(S.s_ids, 128)
-        sent = copy_to(g, core, [H], T.idl[:, 0:L], T.idl[:, L:2 * L], S.r_ids, S.r_sent, topo)
+        ds = direct(rank, T, topo)
+        g.wait_ge(S.s_ido, 16)
+        sent = copy_to(g, core, [H], T.idd[:], T.ido[:], S.r_ids, S.r_sent, topo)
         g.wait_ge(S.s_qt, 1)
-        sent += copy_to(g, core, [H, F], p, p, S.r_plane, S.r_sent, topo)
-        sent += copy_to(g, core, [H, F], c.bitcast(dt.uint8), c.bitcast(dt.uint8), S.r_codes, S.r_sent, topo)
-        sent += send_slots(g, core, direct(rank, T, topo), T, ufirst[0], 1, S["arr%d" % rank], topo)
-        parts()
+        sent += send([H, F], p, S.r_plane)
+        sent += send([H, F], cb, S.r_codes)
+        sent += send(ds, p, S["ap%d" % rank])
+        sent += send(ds, cb, S["ac%d" % rank])
+        part_starts()
         g.wait_ge(S.r_sent, sent)
     else:
-        parts()
+        part_starts()
         sent = relay(g, core, rank, relayed(rank, T, topo)[0], T, topo)
-        for u in range(1, UNITS):
-            for q in units[u]:
-                g.wait_ge(S["arr%d" % q], need[q])
-            sent += send_slots(g, core, [home], T, ufirst[u], len(units[u]), S["fw%d" % u], topo)
+        for i, qs in enumerate(fplane):
+            for q in qs:
+                g.wait_ge(S["ap%d" % q], need[q])
+            sent += send([home], slots(T, slot_of(qs[0], T, topo), len(qs))[1], S["fp%d" % i])
+        for i, qs in enumerate(fcodes):
+            for q in qs:
+                g.wait_ge(S["ac%d" % q], need[q])
+            sent += send([home], slots(T, slot_of(qs[0], T, topo), len(qs))[0].bitcast(dt.uint8), S["fc%d" % i])
         g.wait_ge(S.qv, 1)
         sent += copy_to(g, core, [home], T.vp[:, HT:TOK], T.vp[:, 0:HT], S.r_v, S.r_sent, topo)
         sent += copy_to(g, core, [home], T.vc[:, HT:TOK].bitcast(dt.uint8), T.vc[:, 0:HT].bitcast(dt.uint8), S.r_v, S.r_sent, topo)
@@ -214,20 +218,17 @@ def lookup_core(g, core, rank, is_rank, T, topo):
     v.wait_ge(S.s_hot, 1)
     for b in range(4):
         v.quantize_mx(T.ec[:, 128 * b:128 * b + 128], T.ep[:, 128 * b:128 * b + 128], T.hot[:, 3 - b:3 - b + 512]).then_inc(S.s_qe, 1)
-    if is_rank:
-        v.wait_ge(S.s_ids, 128)
-    else:
-        v.wait_ge(S.r_ids, n16)
+    v.wait_ge(S.s_ids, 128)
+    first = 0 if is_rank else L
     for t in range(4):
-        v.tensor_copy(T.id4[:, L * t:L * t + L], T.idl[:, 0:L]).then_inc(S.s_id4, 1)
+        v.tensor_copy(T.id4[:, L * t:L * t + L], T.idl[:, first:first + L]).then_inc(S.s_id4, 1)
     v.wait_ge(S.s_id4, 4)
-    W = 4 * L
     for q in range(N):
-        v.tensor_scalar(T.hx[:, W * pos[q]:W * pos[q] + W], T.id4[:], HA[q], HB[q], AluOpType.mult, AluOpType.add).then_inc(S.s_hx, 1)
+        v.tensor_scalar(T.hx[:, W * q:W * q + W], T.id4[:], HA[q], HB[q], AluOpType.mult, AluOpType.add).then_inc(S.s_hx, 1)
     v.wait_ge(S.s_hx, N)
     v.tensor_scalar(T.hc[:], T.hx[:], 5, K - 1, AluOpType.logical_shift_right, AluOpType.bitwise_and).then_inc(S.s_hc, 1)
     v.wait_ge(S.s_hc, 1)
-    v.wait_ge(S.s_cst, 2)
+    v.wait_ge(S.s_cst, 1)
     v.tensor_tensor(T.ofs[:], T.hc[:], T.cst[:], AluOpType.add).then_inc(S.s_ofs, 1)
     v.wait_ge(S.s_ofs, 1)
     v.tensor_copy(T.off[:], T.ofs[:]).then_inc(S.s_off, 1)
@@ -237,63 +238,55 @@ def lookup_core(g, core, rank, is_rank, T, topo):
     v.wait_ge(S.s_off, 1)
 
     g.tensor.wait_ge(S.s_qe, 4)
-    for u, qs in enumerate(units):
-        if u == 0 and is_rank:
+    for u, q in enumerate(order):
+        if q == rank and is_rank:
             g.tensor.wait_ge(S.s_qt, 1)
-        elif u == 0:
-            n = count(common(home, [H, F], topo))
-            g.tensor.wait_ge(S.r_plane, n)
-            g.tensor.wait_ge(S.r_codes, n)
+        elif q == rank:
+            g.tensor.wait_ge(S.r_plane, n16)
+            g.tensor.wait_ge(S.r_codes, n16)
         elif is_rank:
-            g.tensor.wait_ge(S["fw%d" % u], 2 * n16)
+            g.tensor.wait_ge(S["fp%d" % [q in qs for qs in fplane].index(True)], n16)
+            g.tensor.wait_ge(S["fc%d" % [q in qs for qs in fcodes].index(True)], n16)
         else:
-            for q in qs:
-                g.tensor.wait_ge(S["arr%d" % q], need[q])
+            g.tensor.wait_ge(S["ap%d" % q], need[q])
+            g.tensor.wait_ge(S["ac%d" % q], need[q])
         if u >= 2:
-            g.tensor.wait_ge(S["cu%d" % (u - 2)], copies(units, u - 2))
-        uc, up = slots(T, ufirst[u], len(qs))
+            g.tensor.wait_ge(S["cu%d" % order[u - 2]], 4)
+        qc, qp = slots(T, slot_of(q, T, topo), 1)
         for b in range(4):
             a = 512 * (4 * (u % 2) + b)
-            g.tensor.matmul_mx(T.ps[:, a:a + K * len(qs)], T.ec[:, 128 * b:128 * b + 128], T.ep[:, 128 * b:128 * b + 128],
-                               uc, up, True, True).then_inc(S["mm%d_%d" % (u, b)], 1)
+            g.tensor.matmul_mx(T.ps[:, a:a + K], T.ec[:, 128 * b:128 * b + 128], T.ep[:, 128 * b:128 * b + 128],
+                               qc, qp, True, True).then_inc(S["mm%d_%d" % (q, b)], 1)
 
-    def bring(eng, u, bs):
-        base = 4 * K * pos[units[u][0]]
-        n = len(units[u])
-        for b in bs[::n]:
-            for x in range(b, b + n):
-                eng.wait_ge(S["mm%d_%d" % (u, x)], 1)
-            a = 512 * (4 * (u % 2) + b)
-            d = base + K * n * b
-            out, in_ = T.dd[:, d:d + K * n * n], T.ps[:, a:a + K * n * n]
+    def bring(eng, q, bs):
+        for b in bs:
+            eng.wait_ge(S["mm%d_%d" % (q, b)], 1)
+            a = 512 * (4 * (order.index(q) % 2) + b)
+            d = 4 * K * q + K * b
             if eng is v:
-                v.tensor_copy(out, in_).then_inc(S["cu%d" % u], 1)
+                v.tensor_copy(T.dd[:, d:d + K], T.ps[:, a:a + K]).then_inc(S["cu%d" % q], 1)
             else:
-                eng.activation(out, in_, ActivationFunctionType.Copy).then_inc(S["cu%d" % u], 1)
+                eng.activation(T.dd[:, d:d + K], T.ps[:, a:a + K], ActivationFunctionType.Copy).then_inc(S["cu%d" % q], 1)
 
-    every, low, high = [0, 1, 2, 3], [0, 1], [2, 3]
-    for u, bs in enumerate([every, every, low, low, every, every]):
-        bring(g.scalar, u, bs)
+    shared = [order[1], seq[1]]
+    for q in order:
+        bring(g.scalar, q, [0, 1] if q in shared else [0, 1, 2, 3])
 
-    seq = list(range(N))
-    if seq[1] in mine:
-        seq[0], seq[1] = seq[1], seq[0]
-    bring(v, 2, high)
+    bring(v, order[1], [2, 3])
     for k, q in enumerate(seq):
         if k == 1:
-            bring(v, 3, high)
-        a, e = win[q]
-        w = W * pos[q]
-        v.wait_ge(S["cu%d" % unit_of[q]], copies(units, unit_of[q]))
+            bring(v, q, [2, 3])
+        win = T.dd[:, 4 * K * q:4 * K * q + 4 * K]
+        v.wait_ge(S["cu%d" % q], 4)
         if k > 0:
             v.wait_ge(S["add%d" % (k - 1)], 1)
         if k == 0:
-            v.tensor_copy(T.acc[:], T.dd[:, a:e].indirect(T.off[:, w:w + W])).then_inc(S["add%d" % k], 1)
+            v.tensor_copy(T.acc[:], win.indirect(T.off[:, W * q:W * q + W])).then_inc(S["add%d" % k], 1)
         elif k < N - 1:
-            v.tensor_tensor(T.acc[:], T.dd[:, a:e].indirect(T.off[:, w:w + W]), T.acc[:], AluOpType.add).then_inc(S["add%d" % k], 1)
+            v.tensor_tensor(T.acc[:], win.indirect(T.off[:, W * q:W * q + W]), T.acc[:], AluOpType.add).then_inc(S["add%d" % k], 1)
         else:
             for t in range(4):
-                v.tensor_tensor(T.vt[:, t:4 * HT:4], T.dd[:, a:e].indirect(T.off[:, w + L * t:w + L * t + L]),
+                v.tensor_tensor(T.vt[:, t:4 * HT:4], win.indirect(T.off[:, W * q + L * t:W * q + L * t + L]),
                                 T.acc[:, HT * t:HT * t + HT], AluOpType.add).then_inc(S.lv, 1)
     v.wait_ge(S.lv, 4)
     v.quantize_mx(T.vc[:, 0:HT], T.vp[:, 0:HT], T.vt[:]).then_inc(S.qv, 1)
@@ -301,7 +294,7 @@ def lookup_core(g, core, rank, is_rank, T, topo):
     if not is_rank:
         return
     g.tensor.wait_ge(S.s_qw, 1)
-    g.tensor.wait_ge(S["cu%d" % (UNITS - 2)], copies(units, UNITS - 2))
+    g.tensor.wait_ge(S["cu%d" % order[N - 2]], 4)
     for h in range(2):
         if h == 0:
             g.tensor.wait_ge(S.qv, 1)
@@ -319,7 +312,3 @@ def lookup_core(g, core, rank, is_rank, T, topo):
     g.scalar.dma_start(T.y[:, HT:TOK], T.yt[:, HT:TOK]).then_inc(S.s_o1, 16)
     g.sync.wait_ge(S.s_o0, 16)
     g.scalar.wait_ge(S.s_o1, 16)
-
-
-def copies(units, u):
-    return 4 // len(units[u])

from concourse.bass import DstId, RemoteDMATransfer
from concourse.mybir import dt, AluOpType, ActivationFunctionType

N, TOK, K = 8, 256, 256
HA = (1237, 1811, 947, 1543, 2017, 733, 1409, 1699)
HB = (40503, 12289, 58111, 3571, 27644, 61007, 19211, 50021)
HT = TOK // 2
L = HT // 16
W = 4 * L

SCRATCH = {
    "codes": ("sbuf", [128, N * K], "float8_e4m3fn_x4"),
    "planes": ("sbuf", [128, N * K], "uint8"),
    "tt": ("sbuf", [128, 4 * K], "bfloat16"),
    "wt": ("sbuf", [128, 512], "bfloat16"),
    "wc": ("sbuf", [128, 128], "float8_e4m3fn_x4"),
    "wp": ("sbuf", [128, 128], "uint8"),
    "ones": ("sbuf", [128, 516], "bfloat16"),
    "hot": ("sbuf", [128, 516], "bfloat16"),
    "ec": ("sbuf", [128, 512], "float8_e4m3fn_x4"),
    "ep": ("sbuf", [128, 512], "uint8"),
    "ido": ("dram", [128, TOK // 128], "int32"),
    "idd": ("dram", [128, TOK // 128], "int32"),
    "idl": ("sbuf", [128, TOK // 16], "int32"),
    "id4": ("sbuf", [128, W], "int32"),
    "hx": ("sbuf", [128, N * W], "int32"),
    "hc": ("sbuf", [128, N * W], "int32"),
    "cst": ("sbuf", [128, N * W], "int32"),
    "ofs": ("sbuf", [128, N * W], "int32"),
    "off": ("sbuf", [128, N * W], "uint16"),
    "dd": ("sbuf", [128, N * 4 * K], "bfloat16"),
    "acc": ("sbuf", [128, 4 * HT], "float32"),
    "vt": ("sbuf", [128, 4 * HT], "bfloat16"),
    "vc": ("sbuf", [128, TOK], "float8_e4m3fn_x4"),
    "vp": ("sbuf", [128, TOK], "uint8"),
    "yt": ("sbuf", [128, TOK], "float32"),
    "ps": ("psum", [128, 8 * 512], "float32"),
}
SEMAPHORES = (["s_tb", "s_ido", "s_ids", "s_w", "s_ones", "s_hot", "s_cst", "s_qt", "s_qe", "s_id4", "s_hx", "s_hc", "s_ofs", "s_off",
               "s_qw", "s_o0", "s_o1", "r_ids", "r_codes", "r_plane", "r_sent", "r_v", "lv", "qv", "ym0", "ym1", "yc0", "yc1"]
              + ["ac%d" % q for q in range(N)] + ["ap%d" % q for q in range(N)] + ["add%d" % k for k in range(N)]
              + ["fp%d" % i for i in range(3)] + ["fc%d" % i for i in range(5)] + ["cu%d" % q for q in range(N)]
              + ["mm%d_%d" % (q, b) for q in range(N) for b in range(4)])


def planes_of(T, topo):
    a = [q for q in range(N) if q == 0 or topo.same_plane(T.cores[0], T.cores[q])]
    return a, [q for q in range(N) if q not in a]


def sides(rank, T, topo):
    a, b = planes_of(T, topo)
    return (a, b) if rank in a else (b, a)


def relays_of(rank, T, topo):
    home = T.cores[rank]
    mine, other = sides(rank, T, topo)
    owners = [x for x in topo.cores_of(home) if x != home and all(topo.may_write(x, T.cores[d]) for d in other)]
    near = [x for x in owners if topo.die(x) == topo.die(home)]
    far = [x for x in owners if topo.die(x) != topo.die(home)]
    return near[0], far[0]


def helper(rank, T, topo):
    return relays_of(rank, T, topo)[0]


def direct(rank, T, topo):
    mine, other = sides(rank, T, topo)
    me = mine.index(rank)
    return [helper(mine[me ^ x], T, topo) for x in (1, 2, 3)]


def relayed(rank, T, topo):
    mine, other = sides(rank, T, topo)
    me = mine.index(rank)
    return [[helper(other[me ^ x], T, topo) for x in xs] for xs in ((0, 1), (2, 3))]


def count(m):
    return bin(m).count("1")


def common(src, dsts, topo):
    m = topo.mask(src, dsts[0])
    for d in dsts:
        m &= topo.mask(src, d)
    return m


def copy_to(g, src, dsts, out, in_, remote_sem, local_sem, topo):
    m = common(src, dsts, topo)
    ids = []
    for d in dsts:
        rid, pid = topo.addr(d, src)
        ids.append(DstId(rid=rid, pnc=pid))
    g.remote_dma_fused([RemoteDMATransfer(dst_ids=ids, dma_engine_mask=m, remote_sem=remote_sem,
                                          srcs=[in_], dsts=[out] * len(dsts))], local_sem=local_sem)
    return count(m)


def slot_of(q, T, topo):
    a, b = planes_of(T, topo)
    return (a + b).index(q)


def slots(T, s, n):
    return T.codes[:, K * s:K * s + K * n], T.planes[:, K * s:K * s + K * n]


def relay(g, core, rank, dsts, T, topo):
    S = T.sem
    c, p = slots(T, slot_of(rank, T, topo), 1)
    n = count(topo.mask(T.cores[rank], core))
    g.wait_ge(S.r_plane, n)
    sent = copy_to(g, core, dsts, p, p, S["ap%d" % rank], S.r_sent, topo)
    g.wait_ge(S.r_codes, n)
    return sent + copy_to(g, core, dsts, c.bitcast(dt.uint8), c.bitcast(dt.uint8), S["ac%d" % rank], S.r_sent, topo)


def rank_program(g, core, T, topo):
    rank = T.rank_of(core)
    if rank is not None:
        lookup_core(g, core, rank, True, T, topo)
        return
    for q, home in enumerate(T.cores):
        if core in topo.cores_of(home):
            H, F = relays_of(q, T, topo)
            if core == H:
                lookup_core(g, core, q, False, T, topo)
            elif core == F:
                sent = relay(g, core, q, relayed(q, T, topo)[1], T, topo)
                g.wait_ge(T.sem.r_sent, sent)


def lookup_core(g, core, rank, is_rank, T, topo):
    S = T.sem
    v = g.vector
    home = T.cores[rank]
    H, F = relays_of(rank, T, topo)
    mine, other = sides(rank, T, topo)
    me = mine.index(rank)
    o = 2 - 2 * (me // 2)
    n16 = count(topo.mask(H, home))

    need = {}
    for q in range(N):
        if q == rank:
            continue
        for src, dsts in [(T.cores[q], direct(q, T, topo))] + list(zip(relays_of(q, T, topo), relayed(q, T, topo))):
            if core in dsts:
                need[q] = count(common(src, dsts, topo))

    seq = list(range(N))
    if seq[1] in mine:
        seq[0], seq[1] = seq[1], seq[0]
    order = [rank]
    order += [q for q in seq if q in mine and q not in order][:1]
    order += [q for q in seq if q not in order]
    fplane = [[mine[me ^ 1]], mine[o:o + 2], other]
    fcodes = [[mine[me ^ 1]], mine[o:o + 2], other[0:1], other[1:2], other[2:4]]
    fcodes.sort(key=lambda qs: min(order.index(q) for q in qs))

    if is_rank:
        g.sync.dma_start(T.tt[:], T.tb[:]).then_inc(S.s_tb, 16)
        g.scalar.dma_start(T.ido[:], T.ids[:]).then_inc(S.s_ido, 16)
    else:
        for eng in (g.sync, g.scalar):
            eng.wait_ge(S.r_ids, n16)
    for k in range(8):
        eng = g.scalar if k % 2 == 0 else g.sync
        eng.dma_start(T.idl[16 * k:16 * k + 16, :], T.ids[:] if is_rank else T.idd[:]).then_inc(S.s_ids, 16)
    if is_rank:
        g.sync.dma_start(T.wt[:], T.w[:]).then_inc(S.s_w, 16)

    def part_starts():
        g.iota(T.cst[:], [[0, N], [K, 4], [0, L]], 0, 0).then_inc(S.s_cst, 1)

    def send(dsts, ap, sem):
        return copy_to(g, core, dsts, ap, ap, sem, S.r_sent, topo)

    g.wait_ge(S.s_ones, 1)
    g.affine_select(T.hot[:], T.ones[:], [[-1, 516]], AluOpType.is_equal, 0.0, 3, 4).then_inc(S.s_hot, 1)
    c, p = slots(T, slot_of(rank, T, topo), 1)
    cb = c.bitcast(dt.uint8)
    if is_rank:
        ds = direct(rank, T, topo)
        g.wait_ge(S.s_ido, 16)
        sent = copy_to(g, core, [H], T.idd[:], T.ido[:], S.r_ids, S.r_sent, topo)
        g.wait_ge(S.s_qt, 1)
        sent += send([H, F], p, S.r_plane)
        sent += send([H, F], cb, S.r_codes)
        sent += send(ds, p, S["ap%d" % rank])
        sent += send(ds, cb, S["ac%d" % rank])
        part_starts()
        g.wait_ge(S.r_sent, sent)
    else:
        part_starts()
        sent = relay(g, core, rank, relayed(rank, T, topo)[0], T, topo)
        for i, qs in enumerate(fplane):
            for q in qs:
                g.wait_ge(S["ap%d" % q], need[q])
            sent += send([home], slots(T, slot_of(qs[0], T, topo), len(qs))[1], S["fp%d" % i])
        for i, qs in enumerate(fcodes):
            for q in qs:
                g.wait_ge(S["ac%d" % q], need[q])
            sent += send([home], slots(T, slot_of(qs[0], T, topo), len(qs))[0].bitcast(dt.uint8), S["fc%d" % i])
        g.wait_ge(S.qv, 1)
        sent += copy_to(g, core, [home], T.vp[:, HT:TOK], T.vp[:, 0:HT], S.r_v, S.r_sent, topo)
        sent += copy_to(g, core, [home], T.vc[:, HT:TOK].bitcast(dt.uint8), T.vc[:, 0:HT].bitcast(dt.uint8), S.r_v, S.r_sent, topo)
        g.wait_ge(S.r_sent, sent)

    v.memset(T.ones[:], 1.0).then_inc(S.s_ones, 1)
    if is_rank:
        v.wait_ge(S.s_tb, 16)
        v.quantize_mx(c, p, T.tt[:]).then_inc(S.s_qt, 1)
    v.wait_ge(S.s_hot, 1)
    for b in range(4):
        v.quantize_mx(T.ec[:, 128 * b:128 * b + 128], T.ep[:, 128 * b:128 * b + 128], T.hot[:, 3 - b:3 - b + 512]).then_inc(S.s_qe, 1)
    v.wait_ge(S.s_ids, 128)
    first = 0 if is_rank else L
    for t in range(4):
        v.tensor_copy(T.id4[:, L * t:L * t + L], T.idl[:, first:first + L]).then_inc(S.s_id4, 1)
    v.wait_ge(S.s_id4, 4)
    for q in range(N):
        v.tensor_scalar(T.hx[:, W * q:W * q + W], T.id4[:], HA[q], HB[q], AluOpType.mult, AluOpType.add).then_inc(S.s_hx, 1)
    v.wait_ge(S.s_hx, N)
    v.tensor_scalar(T.hc[:], T.hx[:], 5, K - 1, AluOpType.logical_shift_right, AluOpType.bitwise_and).then_inc(S.s_hc, 1)
    v.wait_ge(S.s_hc, 1)
    v.wait_ge(S.s_cst, 1)
    v.tensor_tensor(T.ofs[:], T.hc[:], T.cst[:], AluOpType.add).then_inc(S.s_ofs, 1)
    v.wait_ge(S.s_ofs, 1)
    v.tensor_copy(T.off[:], T.ofs[:]).then_inc(S.s_off, 1)
    if is_rank:
        v.wait_ge(S.s_w, 16)
        v.quantize_mx(T.wc[:], T.wp[:], T.wt[:]).then_inc(S.s_qw, 1)
    v.wait_ge(S.s_off, 1)

    g.tensor.wait_ge(S.s_qe, 4)
    for u, q in enumerate(order):
        if q == rank and is_rank:
            g.tensor.wait_ge(S.s_qt, 1)
        elif q == rank:
            g.tensor.wait_ge(S.r_plane, n16)
            g.tensor.wait_ge(S.r_codes, n16)
        elif is_rank:
            g.tensor.wait_ge(S["fp%d" % [q in qs for qs in fplane].index(True)], n16)
            g.tensor.wait_ge(S["fc%d" % [q in qs for qs in fcodes].index(True)], n16)
        else:
            g.tensor.wait_ge(S["ap%d" % q], need[q])
            g.tensor.wait_ge(S["ac%d" % q], need[q])
        if u >= 2:
            g.tensor.wait_ge(S["cu%d" % order[u - 2]], 4)
        qc, qp = slots(T, slot_of(q, T, topo), 1)
        for b in range(4):
            a = 512 * (4 * (u % 2) + b)
            g.tensor.matmul_mx(T.ps[:, a:a + K], T.ec[:, 128 * b:128 * b + 128], T.ep[:, 128 * b:128 * b + 128],
                               qc, qp, True, True).then_inc(S["mm%d_%d" % (q, b)], 1)

    def bring(eng, q, bs):
        for b in bs:
            eng.wait_ge(S["mm%d_%d" % (q, b)], 1)
            a = 512 * (4 * (order.index(q) % 2) + b)
            d = 4 * K * q + K * b
            if eng is v:
                v.tensor_copy(T.dd[:, d:d + K], T.ps[:, a:a + K]).then_inc(S["cu%d" % q], 1)
            else:
                eng.activation(T.dd[:, d:d + K], T.ps[:, a:a + K], ActivationFunctionType.Copy).then_inc(S["cu%d" % q], 1)

    shared = [order[1], seq[1]]
    for q in order:
        bring(g.scalar, q, [0, 1] if q in shared else [0, 1, 2, 3])

    bring(v, order[1], [2, 3])
    for k, q in enumerate(seq):
        if k == 1:
            bring(v, q, [2, 3])
        win = T.dd[:, 4 * K * q:4 * K * q + 4 * K]
        v.wait_ge(S["cu%d" % q], 4)
        if k > 0:
            v.wait_ge(S["add%d" % (k - 1)], 1)
        if k == 0:
            v.tensor_copy(T.acc[:], win.indirect(T.off[:, W * q:W * q + W])).then_inc(S["add%d" % k], 1)
        elif k < N - 1:
            v.tensor_tensor(T.acc[:], win.indirect(T.off[:, W * q:W * q + W]), T.acc[:], AluOpType.add).then_inc(S["add%d" % k], 1)
        else:
            for t in range(4):
                v.tensor_tensor(T.vt[:, t:4 * HT:4], win.indirect(T.off[:, W * q + L * t:W * q + L * t + L]),
                                T.acc[:, HT * t:HT * t + HT], AluOpType.add).then_inc(S.lv, 1)
    v.wait_ge(S.lv, 4)
    v.quantize_mx(T.vc[:, 0:HT], T.vp[:, 0:HT], T.vt[:]).then_inc(S.qv, 1)

    if not is_rank:
        return
    g.tensor.wait_ge(S.s_qw, 1)
    g.tensor.wait_ge(S["cu%d" % order[N - 2]], 4)
    for h in range(2):
        if h == 0:
            g.tensor.wait_ge(S.qv, 1)
        else:
            g.tensor.wait_ge(S.r_v, 2 * n16)
        g.tensor.matmul_mx(T.ps[:, 512 * h:512 * h + HT], T.wc[:], T.wp[:], T.vc[:, HT * h:HT * h + HT], T.vp[:, HT * h:HT * h + HT],
                           True, True).then_inc(S["ym%d" % h], 1)
    v.wait_ge(S.ym0, 1)
    v.tensor_copy(T.yt[:, 0:HT], T.ps[:, 0:HT]).then_inc(S.yc0, 1)
    g.sync.wait_ge(S.yc0, 1)
    g.sync.dma_start(T.y[:, 0:HT], T.yt[:, 0:HT]).then_inc(S.s_o0, 16)
    g.scalar.wait_ge(S.ym1, 1)
    g.scalar.activation(T.yt[:, HT:TOK], T.ps[:, 512:512 + HT], ActivationFunctionType.Copy).then_inc(S.yc1, 1)
    g.scalar.wait_ge(S.yc1, 1)
    g.scalar.dma_start(T.y[:, HT:TOK], T.yt[:, HT:TOK]).then_inc(S.s_o1, 16)
    g.sync.wait_ge(S.s_o0, 16)
    g.scalar.wait_ge(S.s_o1, 16)
